import numpy as np
import ml_dtypes


def mxq(x, axis, fmt="e4m3"):
    dtype, down = {"e4m3": (ml_dtypes.float8_e4m3fn, 7), "e5m2": (ml_dtypes.float8_e5m2, 14)}[fmt]
    v = np.moveaxis(np.asarray(x, np.float32).astype(ml_dtypes.bfloat16).astype(np.float64), axis, -1)
    blocks = v.reshape(v.shape[:-1] + (-1, 32))
    amax = np.abs(blocks).max(-1, keepdims=True)
    byte = np.maximum(np.where(amax > 0, np.frexp(amax)[1] - 1 + 127, 0) - down, 1)
    scale = np.exp2(byte - 127.0)
    codes = (blocks / scale).astype(np.float32).astype(dtype).astype(np.float64)
    return np.moveaxis((codes * scale).reshape(v.shape), -1, axis)


WIDE = False


def mx_kscale(k):
    if not WIDE:
        return np.ones(k)
    levels = np.array([10, -10, 5, -5, 0])
    if k % 512:
        return np.exp2(np.random.permutation(np.resize(levels, k // 32))).repeat(32)
    a = np.empty((k // 512, 16))
    for p in range(k // 512):
        a[p, :8] = np.random.permutation(np.resize(levels, 8))
        for g in range(8):
            far = levels[np.abs(levels - a[p, g]) >= 10]
            a[p, g + 8] = far[np.random.randint(len(far))]
    return np.exp2(a.ravel()).repeat(32)


def f64(x):
    return np.asarray(x).astype(np.float64)


def striped(idx):
    return np.tile(idx.reshape(-1, 16).T, (8, 1)).astype(np.uint16)


def unstriped(offs):
    return offs[:16].T.reshape(-1).astype(np.int64)


def striped8(idx):
    return np.concatenate([x.reshape(-1, 16).T for x in idx]).astype(np.uint16)


def runs(offs, k):
    lists = np.stack([offs[16 * r : 16 * r + 16].T.reshape(-1) for r in range(8)]).astype(np.int64)
    return lists[np.arange(k) % 512 // 64]


def pack_weight(w):
    k, n = w.shape
    w = f64(np.asarray(w, np.float32).astype(ml_dtypes.bfloat16)).reshape(k // 32, 32, n)
    amax = np.abs(w).max(1)
    byte = np.clip(np.where(amax > 0, np.frexp(amax)[1] - 1 + 127 - 7, 1), 1, 254)
    scaled = (w * np.exp2(127.0 - byte)[:, None, :]).reshape(k, n).astype(np.float32)
    words = np.ascontiguousarray(scaled.reshape(k // 512, 128, 4, n).transpose(0, 1, 3, 2)).astype(ml_dtypes.float8_e4m3fn).view(np.uint8)
    return words, np.ascontiguousarray(byte.astype(np.uint8).reshape(k // 512, 16, n))


def unpack_weight(words, scales):
    g, p, n, _ = words.shape
    vals = np.ascontiguousarray(words).view(ml_dtypes.float8_e4m3fn).astype(np.float64) * np.repeat(np.exp2(scales.astype(np.float64) - 127.0), 8, axis=1)[..., None]
    return vals.transpose(0, 1, 3, 2).reshape(g * 512, n)

def planes(y):
    n, m = y.shape
    v = y.astype(np.float32).astype(ml_dtypes.bfloat16).astype(np.float64).reshape(n // 32, 32, m)
    top = np.abs(v).max(1)
    byte = np.clip(np.where(top > 0, np.frexp(top)[1] - 1 + 127 - 7, 1), 1, 254)
    codes = (v * np.exp2(127.0 - byte)[:, None, :]).reshape(n, m).astype(np.float32).astype(ml_dtypes.float8_e4m3fn).view(np.uint8)
    words = codes.reshape(n // 512, 128, 4, m).transpose(0, 1, 3, 2)
    return np.ascontiguousarray(words), np.ascontiguousarray(byte.astype(np.uint8).reshape(n // 512, 16, m))


K, T, S, H, C = 512, 2048, 512, 512, 512


def setup_inputs():
    n = np.random.standard_normal
    s = mx_kscale(K)[:, None]
    packed_xT = pack_weight(n((K, T)) * s)
    packed_w1 = pack_weight(n((K, H)) / np.sqrt(K) / s)
    return {
        "x_words": packed_xT[0],
        "x_scales": packed_xT[1],
        "w1_words": packed_w1[0],
        "w1_scales": packed_w1[1],
        "gs": (np.random.uniform(0.5, 1.5, (K, 1)) / s).astype(np.float32),
        "offs": striped(np.random.permutation(T)[:S]),
        "n1": striped8(np.stack([np.random.permutation(S) for _ in range(8)])),
        "n2": striped8(np.stack([np.random.permutation(S) for _ in range(8)])),
        "cand": striped(np.random.permutation(T)[:C]),
        "n3": striped8(np.stack([np.random.permutation(S) for _ in range(8)])),
        "n4": striped8(np.stack([np.random.permutation(S) for _ in range(8)])),
    }


def reference(x_words, x_scales, w1_words, w1_scales, gs, offs, n1, n2, cand, n3, n4):
    x_cand = unpack_weight(x_words, x_scales)[:, unstriped(cand)]
    xq = unpack_weight(x_words, x_scales)[:, unstriped(offs)]
    y = unpack_weight(w1_words, w1_scales).T @ xq
    sq = (y) ** 2
    z = f64(gs) * ((y[np.arange(H)[:, None], runs(n2, H)]) / (np.sqrt(sq + sq[np.arange(H)[:, None], runs(n1, H)] + 0.25)))
    s = 0.0625 * ((x_cand.T @ mxq(z, 0, "e4m3")))
    out_0 = (s * (s[np.arange(C)[:, None], runs(n3, C)])) * (np.tanh(s[np.arange(C)[:, None], runs(n4, C)]))
    return (out_0,) + planes(out_0)

@@ -1,0 +1,192 @@
+from contextlib import ExitStack
+
+import concourse.mybir as mybir
+
+F32 = mybir.dt.float32
+BF16 = mybir.dt.bfloat16
+I32 = mybir.dt.int32
+U32 = mybir.dt.uint32
+U16 = mybir.dt.uint16
+U8 = mybir.dt.uint8
+FP8X4 = mybir.dt.float8_e4m3fn_x4
+ACT = mybir.ActivationFunctionType
+ALU = mybir.AluOpType
+
+P = 128
+PACK = 4
+T = 2048
+S = 512
+FLOPS = 2 * 2 * 512 * 512 * 512
+Z_PIECES = ((0, 256), (256, 128), (384, 128))
+O_PIECES = ((0, 256), (256, 128), (384, 128))
+HALVES = ((0, 256), (256, 256))
+
+
+def tile_picked_candrmscube_none_po_kernel(
+    tc, x_words, x_scales, w1_words, w1_scales, gs, offs, n1, n2, cand, n3, n4, out_0, out_1, out_2
+):
+    nc = tc.nc
+    with ExitStack() as ctx:
+        keep = ctx.enter_context(tc.tile_pool(name="keep", bufs=1))
+        psum = ctx.enter_context(tc.psum_pool(name="psum", bufs=1))
+
+        def sb(name, shape, dtype, tag=None):
+            return keep.tile(shape, dtype, name=name, tag=tag or name, align_bytes=64)
+
+        def load_list(name, src):
+            tile = keep.tile([P, S // 16], U16, name=name)
+            nc.sync.dma_start(tile[:], src)
+            return tile
+
+        def cols(lst, j0, w):
+            return lst[:, j0 // 16 : (j0 + w) // 16]
+
+        def load_scale_rows(queue, tile, src):
+            for q in range(4):
+                queue.dma_start(tile[32 * q : 32 * q + 4, :].bitcast(I32), src[0, 4 * q : 4 * q + 4, :].bitcast(I32))
+
+        def deal(dst, src, t0, t1):
+            nc.vector.tensor_copy(
+                dst.rearrange("p (t m) -> p t m", m=P), src.rearrange("p (m t) -> p t m", t=PACK)[:, t0:t1, :]
+            )
+
+        def interleave(engine_copy, name, src, w):
+            dst = sb(name, [P, w * PACK], BF16)
+            engine_copy(dst[:].rearrange("p (j t) -> p j t", t=PACK), src[:].rearrange("p t j -> p j t"))
+            return dst
+
+        xs = sb("xs", [P, T], U8)
+        ws = sb("ws", [P, S], U8)
+        quarter = sb("quarter", [P, 1], F32)
+        warm = sb("warm", [P, 1], F32)
+        nc.vector.memset(xs[:].bitcast(I32), 0)
+        nc.gpsimd.memset(ws[:].bitcast(I32), 0)
+        nc.gpsimd.memset(quarter[:], 0.25)
+
+        ww = sb("ww", [P, S], I32)
+        xw = sb("xw", [P, T], I32)
+        gain = sb("gain", [P, PACK], F32)
+        l_offs = load_list("l_offs", offs)
+        nc.scalar.dma_start(ww[:], w1_words[0].rearrange("p n t -> p (n t)").bitcast(I32))
+        nc.scalar.activation(warm[:], quarter[:], ACT.Abs_reciprocal_sqrt)
+        load_scale_rows(nc.sync, xs, x_scales)
+        nc.sync.dma_start(xw[:], x_words[0].rearrange("p n t -> p (n t)").bitcast(I32))
+        load_scale_rows(nc.sync, ws, w1_scales)
+        l_cand = load_list("l_cand", cand)
+        l_n1 = load_list("l_n1", n1)
+        nc.sync.dma_start(gain[:], gs.rearrange("(p t) o -> p (t o)", t=PACK))
+        l_n2 = load_list("l_n2", n2)
+        l_n3 = load_list("l_n3", n3)
+        l_n4 = load_list("l_n4", n4)
+
+        wwd = sb("wwd", [P, S], U32)
+        wsd = sb("wsd", [P, S], U8)
+        deal(wwd[:], ww[:].bitcast(U32), 0, PACK)
+        tok_s = sb("tok_s", [P, S], U8)
+        tok_w = sb("tok_w", [P, S], U32)
+        can_s = sb("can_s", [P, S], U8)
+        can_w = sb("can_w", [P, S], U32)
+        nc.vector.tensor_copy(tok_s[:], xs[:].indirect(l_offs[:]))
+        deal(wsd[:], ws[:], 0, PACK)
+        nc.vector.tensor_copy(tok_w[:], xw[:].bitcast(U32).indirect(l_offs[:]))
+
+        y_ps = [psum.tile([P, S], F32, name=f"y_ps{t}", tag=f"bank{t}") for t in range(PACK)]
+        for t in range(PACK):
+            m = slice(P * t, P * (t + 1))
+            nc.tensor.matmul_mx(
+                y_ps[t][:], lhsT=wwd[:, m].bitcast(FP8X4), lhsT_scale=wsd[:, m],
+                rhs=tok_w[:].bitcast(FP8X4), rhs_scale=tok_s[:], start=True, stop=True,
+            )
+
+        nc.vector.tensor_copy(can_s[:], xs[:].indirect(l_cand[:]))
+        nc.vector.tensor_copy(can_w[:], xw[:].bitcast(U32).indirect(l_cand[:]))
+        can_sd0 = sb("can_sd0", [P, P], U8)
+        can_wd0 = sb("can_wd0", [P, P], U32)
+        deal(can_wd0[:], can_w[:], 0, 1)
+        deal(can_sd0[:], can_s[:], 0, 1)
+
+        sq = [sb(f"sq{t}", [P, S], F32) for t in range(PACK)]
+        sq2 = [sb(f"sq2_{t}", [P, S], F32) for t in range(PACK)]
+        gy = [sb(f"gy{t}", [P, S], F32) for t in range(PACK)]
+        den = [sb(f"den{t}", [P, S], F32) for t in range(PACK)]
+        inv = [sb(f"inv{t}", [P, S], F32) for t in range(PACK)]
+        for t in range(PACK):
+            nc.scalar.activation(sq[t][:], y_ps[t][:], ACT.Square)
+            nc.scalar.activation(sq2[t][:], y_ps[t][:], ACT.Square)
+            for j0, w in HALVES:
+                nc.vector.tensor_tensor(
+                    den[t][:, j0 : j0 + w], sq[t][:].indirect(cols(l_n1, j0, w)), sq2[t][:, j0 : j0 + w], ALU.add
+                )
+        for t in range(PACK):
+            nc.scalar.activation(gy[t][:], y_ps[t][:], ACT.Copy, scale=gain[:, t : t + 1])
+            nc.scalar.activation(inv[t][:], den[t][:], ACT.Abs_reciprocal_sqrt, bias=quarter[:])
+        nc.scalar.activation(warm[:], inv[PACK - 1][:, 0:1], ACT.Tanh)
+
+        zq = sb("zq", [P, S], U32)
+        zs = sb("zs", [P, S], U8)
+        s0_ps = []
+        for h, (j0, w) in enumerate(Z_PIECES):
+            z = sb(f"z{h}", [P, PACK, w], F32)
+            for t in range(PACK):
+                nc.vector.tensor_tensor(
+                    z[:, t, :], gy[t][:].indirect(cols(l_n2, j0, w)), inv[t][:, j0 : j0 + w], ALU.mult
+                )
+            last = h == len(Z_PIECES) - 1
+            zb = interleave(nc.vector.tensor_copy if last else nc.scalar.copy, f"zb{h}", z, w)
+            nc.vector.quantize_mx(zq[:, j0 : j0 + w].bitcast(FP8X4), zs[:, j0 : j0 + w], zb[:])
+            bank = psum.tile([P, w], F32, name=f"s0_ps{h}", tag=f"bank{PACK + h}")
+            nc.tensor.matmul_mx(
+                bank[:], lhsT=can_wd0[:].bitcast(FP8X4), lhsT_scale=can_sd0[:],
+                rhs=zq[:, j0 : j0 + w].bitcast(FP8X4), rhs_scale=zs[:, j0 : j0 + w], start=True, stop=True,
+            )
+            s0_ps.append(bank)
+
+        can_wd = sb("can_wd", [P, (PACK - 1) * P], U32, tag=f"zb{len(Z_PIECES) - 1}")
+        can_sd = sb("can_sd", [P, (PACK - 1) * P], U8, tag=f"z{len(Z_PIECES) - 1}")
+        deal(can_wd[:], can_w[:], 1, PACK)
+        deal(can_sd[:], can_s[:], 1, PACK)
+        parts = [[(s0_ps[h][:], j0, w) for h, (j0, w) in enumerate(Z_PIECES)]]
+        for t in range(1, PACK):
+            m = slice(P * (t - 1), P * t)
+            bank = psum.tile([P, S], F32, name=f"s_ps{t}", tag=f"bank{t}")
+            nc.tensor.matmul_mx(
+                bank[:], lhsT=can_wd[:, m].bitcast(FP8X4), lhsT_scale=can_sd[:, m],
+                rhs=zq[:].bitcast(FP8X4), rhs_scale=zs[:], start=True, stop=True,
+            )
+            parts.append([(bank[:], 0, S)])
+        out_rows = out_0.rearrange("(p t) j -> p t j", t=PACK)
+        out_words = out_1[0].rearrange("p n t -> p (n t)").bitcast(I32)
+        o_s = sb("o_s", [P, S], U8)
+
+        sw = [sb(f"sw{t}", [P, S], F32) for t in range(PACK)]
+        s2 = [sb(f"s2_{t}", [P, S], F32) for t in range(PACK)]
+        th = [sb(f"th{t}", [P, S], F32) for t in range(PACK)]
+        a = [sb(f"a{t}", [P, S], F32) for t in range(PACK)]
+
+        def out_of_bank(dst, t, func):
+            for src, j0, w in parts[t]:
+                nc.scalar.activation(dst[:, j0 : j0 + w], src, func, scale=0.0625)
+
+        for t in range(PACK):
+            out_of_bank(sw[t], t, ACT.Copy)
+            out_of_bank(s2[t], t, ACT.Copy)
+            for j0, w in HALVES:
+                nc.vector.tensor_tensor(
+                    a[t][:, j0 : j0 + w], sw[t][:].indirect(cols(l_n3, j0, w)), s2[t][:, j0 : j0 + w], ALU.mult
+                )
+            if t > 0:
+                out_of_bank(th[t - 1], t - 1, ACT.Tanh)
+        out_of_bank(th[PACK - 1], PACK - 1, ACT.Tanh)
+        for h, (j0, w) in enumerate(O_PIECES):
+            o = sb(f"o{h}", [P, PACK, w], F32)
+            for t in range(PACK):
+                nc.vector.tensor_tensor(o[:, t, :], th[t][:].indirect(cols(l_n4, j0, w)), a[t][:, j0 : j0 + w], ALU.mult)
+            nc.sync.dma_start(out_rows[:, :, j0 : j0 + w], o[:])
+            last = h == len(O_PIECES) - 1
+            ob = interleave(nc.vector.tensor_copy if last else nc.scalar.copy, f"ob{h}", o, w)
+            oq = sb(f"oq{h}", [P, w], U32)
+            nc.vector.quantize_mx(oq[:].bitcast(FP8X4), o_s[:, j0 : j0 + w], ob[:])
+            nc.scalar.dma_start(out_words[:, j0 : j0 + w], oq[:].bitcast(I32))
+        for q in range(4):
+            queue = nc.sync if q % 2 == 0 else nc.scalar
+            queue.dma_start(out_2[0, 4 * q : 4 * q + 4, :].bitcast(I32), o_s[32 * q : 32 * q + 4, :].bitcast(I32))

@@ -16,10 +16,13 @@ P = 128
 PACK = 4
 T = 2048
 S = 512
+HALF = S // 2
+EARLY = 1
 FLOPS = 2 * 2 * 512 * 512 * 512
+HALVES = ((0, HALF), (HALF, HALF))
 Z_PIECES = ((0, 256), (256, 128), (384, 128))
-O_PIECES = ((0, 256), (256, 128), (384, 128))
-HALVES = ((0, 256), (256, 256))
+O_PIECES = HALVES
+SCALAR_COLS = 96
 
 
 def tile_picked_candrmscube_none_po_kernel(
@@ -50,77 +53,116 @@ def tile_picked_candrmscube_none_po_kernel(
                 dst.rearrange("p (t m) -> p t m", m=P), src.rearrange("p (m t) -> p t m", t=PACK)[:, t0:t1, :]
             )
 
+        def deal_words(dst, src, t0, t1):
+            nc.vector.tensor_copy(
+                dst.rearrange("p (t m) -> p m t", m=P), src.rearrange("p (m t) -> p m t", t=PACK)[:, :, t0:t1]
+            )
+
         def interleave(engine_copy, name, src, w):
             dst = sb(name, [P, w * PACK], BF16)
-            engine_copy(dst[:].rearrange("p (j t) -> p j t", t=PACK), src[:].rearrange("p t j -> p j t"))
+            engine_copy(
+                dst[:].rearrange("p (c i t) -> p c t i", i=4, t=PACK), src[:].rearrange("p t (c i) -> p c t i", i=4)
+            )
             return dst
+
+        def chained(name):
+            tiles = [sb(f"{name}{t}", [P, S if t in (0, PACK) else 2 * S], F32) for t in range(PACK + 1)]
+            windows = tiles[:PACK]
+            first = [tiles[t][:, 0:S] for t in range(PACK)]
+            second = [tiles[t + 1][:, S : 2 * S] if t + 1 < PACK else tiles[PACK][:] for t in range(PACK)]
+            return windows, first, second
+
+        def fused(dst, window, lst, other, op, whole):
+            if whole:
+                nc.vector.tensor_tensor(dst, window[:].indirect(lst[:]), other, op)
+            else:
+                for j0, w in HALVES:
+                    nc.vector.tensor_tensor(
+                        dst[:, j0 : j0 + w], window[:].indirect(cols(lst, j0, w)), other[:, j0 : j0 + w], op
+                    )
+
+        def probe(name, ap, dtype):
+            clock = sb(name, [P, 1], dtype)
+            nc.gpsimd.tensor_copy(clock[:], ap)
 
         xs = sb("xs", [P, T], U8)
         ws = sb("ws", [P, S], U8)
         quarter = sb("quarter", [P, 1], F32)
         warm = sb("warm", [P, 1], F32)
-        nc.vector.memset(xs[:].bitcast(I32), 0)
-        nc.gpsimd.memset(ws[:].bitcast(I32), 0)
-        nc.gpsimd.memset(quarter[:], 0.25)
+        nc.gpsimd.memset(xs[:].bitcast(I32), 0)
+        nc.vector.memset(ws[:].bitcast(I32), 0)
+        nc.vector.memset(quarter[:], 0.25)
 
         ww = sb("ww", [P, S], I32)
         xw = sb("xw", [P, T], I32)
         gain = sb("gain", [P, PACK], F32)
         l_offs = load_list("l_offs", offs)
-        nc.scalar.dma_start(ww[:], w1_words[0].rearrange("p n t -> p (n t)").bitcast(I32))
+        l_cand = load_list("l_cand", cand)
+        nc.sync.dma_start(ww[:], w1_words[0].rearrange("p n t -> p (n t)").bitcast(I32))
         nc.scalar.activation(warm[:], quarter[:], ACT.Abs_reciprocal_sqrt)
         load_scale_rows(nc.sync, xs, x_scales)
         nc.sync.dma_start(xw[:], x_words[0].rearrange("p n t -> p (n t)").bitcast(I32))
         load_scale_rows(nc.sync, ws, w1_scales)
-        l_cand = load_list("l_cand", cand)
         l_n1 = load_list("l_n1", n1)
         nc.sync.dma_start(gain[:], gs.rearrange("(p t) o -> p (t o)", t=PACK))
         l_n2 = load_list("l_n2", n2)
-        l_n3 = load_list("l_n3", n3)
         l_n4 = load_list("l_n4", n4)
+        l_n3 = load_list("l_n3", n3)
 
         wwd = sb("wwd", [P, S], U32)
         wsd = sb("wsd", [P, S], U8)
-        deal(wwd[:], ww[:].bitcast(U32), 0, PACK)
+        deal_words(wwd[:], ww[:].bitcast(U32), 0, PACK)
         tok_s = sb("tok_s", [P, S], U8)
         tok_w = sb("tok_w", [P, S], U32)
         can_s = sb("can_s", [P, S], U8)
-        can_w = sb("can_w", [P, S], U32)
         nc.vector.tensor_copy(tok_s[:], xs[:].indirect(l_offs[:]))
-        deal(wsd[:], ws[:], 0, PACK)
+        nc.vector.tensor_copy(can_s[:], xs[:].indirect(l_cand[:]))
         nc.vector.tensor_copy(tok_w[:], xw[:].bitcast(U32).indirect(l_offs[:]))
+        deal(wsd[:], ws[:], 0, PACK)
 
-        y_ps = [psum.tile([P, S], F32, name=f"y_ps{t}", tag=f"bank{t}") for t in range(PACK)]
+        y_parts = []
         for t in range(PACK):
             m = slice(P * t, P * (t + 1))
-            nc.tensor.matmul_mx(
-                y_ps[t][:], lhsT=wwd[:, m].bitcast(FP8X4), lhsT_scale=wsd[:, m],
-                rhs=tok_w[:].bitcast(FP8X4), rhs_scale=tok_s[:], start=True, stop=True,
-            )
-
-        nc.vector.tensor_copy(can_s[:], xs[:].indirect(l_cand[:]))
-        nc.vector.tensor_copy(can_w[:], xw[:].bitcast(U32).indirect(l_cand[:]))
-        can_sd0 = sb("can_sd0", [P, P], U8)
-        can_wd0 = sb("can_wd0", [P, P], U32)
-        deal(can_wd0[:], can_w[:], 0, 1)
-        deal(can_sd0[:], can_s[:], 0, 1)
-
-        sq = [sb(f"sq{t}", [P, S], F32) for t in range(PACK)]
-        sq2 = [sb(f"sq2_{t}", [P, S], F32) for t in range(PACK)]
-        gy = [sb(f"gy{t}", [P, S], F32) for t in range(PACK)]
-        den = [sb(f"den{t}", [P, S], F32) for t in range(PACK)]
-        inv = [sb(f"inv{t}", [P, S], F32) for t in range(PACK)]
-        for t in range(PACK):
-            nc.scalar.activation(sq[t][:], y_ps[t][:], ACT.Square)
-            nc.scalar.activation(sq2[t][:], y_ps[t][:], ACT.Square)
-            for j0, w in HALVES:
-                nc.vector.tensor_tensor(
-                    den[t][:, j0 : j0 + w], sq[t][:].indirect(cols(l_n1, j0, w)), sq2[t][:, j0 : j0 + w], ALU.add
+            y_parts.append([])
+            for h, (j0, w) in enumerate(HALVES if t == 0 else ((0, S),)):
+                bank = psum.tile([P, w], F32, name=f"y_ps{t}_{h}", tag=f"bank{t + 7 * h}")
+                nc.tensor.matmul_mx(
+                    bank[:], lhsT=wwd[:, m].bitcast(FP8X4), lhsT_scale=wsd[:, m],
+                    rhs=tok_w[:, j0 : j0 + w].bitcast(FP8X4), rhs_scale=tok_s[:, j0 : j0 + w], start=True, stop=True,
                 )
+                y_parts[t].append((bank[:], j0, w))
+
+        can_w = sb("can_w", [P, S], U32, tag="ws")
+        nc.vector.tensor_copy(can_w[:], xw[:].bitcast(U32).indirect(l_cand[:]))
+        can_sd0 = sb("can_sd0", [P, EARLY * P], U8)
+        can_wd0 = sb("can_wd0", [P, EARLY * P], U32)
+        deal(can_sd0[:], can_s[:], 0, EARLY)
+        deal_words(can_wd0[:], can_w[:], 0, EARLY)
+
+        sq_win, sq, sq2 = chained("sq")
+        gy = [sb(f"gy{t}", [P, S], F32) for t in range(PACK)]
+        th_win = [sb(f"th{t}", [P, 2 * S], F32) for t in range(PACK)]
+        th = [th_win[t][:, 0:S] for t in range(PACK)]
+        den = [th_win[t][:, S : 2 * S] for t in range(PACK)]
+        inv = [sb(f"inv{t}", [P, S], F32) for t in range(PACK - 1)]
+        inv_last = [sb(f"inv_last{h}", [P, w], F32, tag=f"z{h + 1}") for h, (j0, w) in enumerate(Z_PIECES)]
         for t in range(PACK):
-            nc.scalar.activation(gy[t][:], y_ps[t][:], ACT.Copy, scale=gain[:, t : t + 1])
-            nc.scalar.activation(inv[t][:], den[t][:], ACT.Abs_reciprocal_sqrt, bias=quarter[:])
-        nc.scalar.activation(warm[:], inv[PACK - 1][:, 0:1], ACT.Tanh)
+            for src, j0, w in y_parts[t]:
+                nc.scalar.activation(sq[t][:, j0 : j0 + w], src, ACT.Square)
+                nc.scalar.activation(sq2[t][:, j0 : j0 + w], src, ACT.Square)
+        for t in range(PACK):
+            fused(den[t], sq_win[t], l_n1, sq2[t], ALU.add, t > 0)
+        for h, (j0, w) in enumerate(HALVES):
+            for t in range(PACK):
+                if h == 0:
+                    for src, k0, v in y_parts[t]:
+                        nc.scalar.activation(gy[t][:, k0 : k0 + v], src, ACT.Copy, scale=gain[:, t : t + 1])
+                if t < PACK - 1:
+                    spans = [(inv[t][:, j0 : j0 + w], j0, w)]
+                else:
+                    spans = [(inv_last[g][:], k0, v) for g, (k0, v) in enumerate(Z_PIECES) if j0 <= k0 < j0 + w]
+                for dst, k0, v in spans:
+                    nc.scalar.activation(dst, den[t][:, k0 : k0 + v], ACT.Abs_reciprocal_sqrt, bias=quarter[:])
 
         zq = sb("zq", [P, S], U32)
         zs = sb("zs", [P, S], U8)
@@ -128,29 +170,31 @@ def tile_picked_candrmscube_none_po_kernel(
         for h, (j0, w) in enumerate(Z_PIECES):
             z = sb(f"z{h}", [P, PACK, w], F32)
             for t in range(PACK):
-                nc.vector.tensor_tensor(
-                    z[:, t, :], gy[t][:].indirect(cols(l_n2, j0, w)), inv[t][:, j0 : j0 + w], ALU.mult
-                )
+                factor = inv[t][:, j0 : j0 + w] if t < PACK - 1 else inv_last[h][:]
+                nc.vector.tensor_tensor(z[:, t, :], gy[t][:].indirect(cols(l_n2, j0, w)), factor, ALU.mult)
             last = h == len(Z_PIECES) - 1
             zb = interleave(nc.vector.tensor_copy if last else nc.scalar.copy, f"zb{h}", z, w)
+            if h == 1:
+                nc.scalar.activation(warm[:], zb[:, 0:1], ACT.Tanh)
             nc.vector.quantize_mx(zq[:, j0 : j0 + w].bitcast(FP8X4), zs[:, j0 : j0 + w], zb[:])
             bank = psum.tile([P, w], F32, name=f"s0_ps{h}", tag=f"bank{PACK + h}")
             nc.tensor.matmul_mx(
-                bank[:], lhsT=can_wd0[:].bitcast(FP8X4), lhsT_scale=can_sd0[:],
+                bank[:], lhsT=can_wd0[:, 0:P].bitcast(FP8X4), lhsT_scale=can_sd0[:, 0:P],
                 rhs=zq[:, j0 : j0 + w].bitcast(FP8X4), rhs_scale=zs[:, j0 : j0 + w], start=True, stop=True,
             )
             s0_ps.append(bank)
 
-        can_wd = sb("can_wd", [P, (PACK - 1) * P], U32, tag=f"zb{len(Z_PIECES) - 1}")
-        can_sd = sb("can_sd", [P, (PACK - 1) * P], U8, tag=f"z{len(Z_PIECES) - 1}")
-        deal(can_wd[:], can_w[:], 1, PACK)
-        deal(can_sd[:], can_s[:], 1, PACK)
+        can_wd = sb("can_wd", [P, (PACK - EARLY) * P], U32, tag="zb2")
+        can_sd = sb("can_sd", [P, (PACK - EARLY) * P], U8, tag="z2")
+        deal(can_sd[:], can_s[:], EARLY, PACK)
+        deal_words(can_wd[:], can_w[:], EARLY, PACK)
         parts = [[(s0_ps[h][:], j0, w) for h, (j0, w) in enumerate(Z_PIECES)]]
         for t in range(1, PACK):
-            m = slice(P * (t - 1), P * t)
+            words, scales, u = (can_wd0, can_sd0, t) if t < EARLY else (can_wd, can_sd, t - EARLY)
+            m = slice(P * u, P * (u + 1))
             bank = psum.tile([P, S], F32, name=f"s_ps{t}", tag=f"bank{t}")
             nc.tensor.matmul_mx(
-                bank[:], lhsT=can_wd[:, m].bitcast(FP8X4), lhsT_scale=can_sd[:, m],
+                bank[:], lhsT=words[:, m].bitcast(FP8X4), lhsT_scale=scales[:, m],
                 rhs=zq[:].bitcast(FP8X4), rhs_scale=zs[:], start=True, stop=True,
             )
             parts.append([(bank[:], 0, S)])
@@ -158,35 +202,44 @@ def tile_picked_candrmscube_none_po_kernel(
         out_words = out_1[0].rearrange("p n t -> p (n t)").bitcast(I32)
         o_s = sb("o_s", [P, S], U8)
 
-        sw = [sb(f"sw{t}", [P, S], F32) for t in range(PACK)]
-        s2 = [sb(f"s2_{t}", [P, S], F32) for t in range(PACK)]
-        th = [sb(f"th{t}", [P, S], F32) for t in range(PACK)]
-        a = [sb(f"a{t}", [P, S], F32) for t in range(PACK)]
-
-        def out_of_bank(dst, t, func):
-            for src, j0, w in parts[t]:
-                nc.scalar.activation(dst[:, j0 : j0 + w], src, func, scale=0.0625)
-
+        s = [sb(f"s{t}", [P, S], F32) for t in range(PACK)]
+        a = [sb(f"a{t}", [P, S], F32) for t in range(PACK - 1)]
+        a_last = [sb(f"a_last{h}", [P, w], F32, tag=f"o{h + 1}") for h, (j0, w) in enumerate(O_PIECES)]
         for t in range(PACK):
-            out_of_bank(sw[t], t, ACT.Copy)
-            out_of_bank(s2[t], t, ACT.Copy)
-            for j0, w in HALVES:
-                nc.vector.tensor_tensor(
-                    a[t][:, j0 : j0 + w], sw[t][:].indirect(cols(l_n3, j0, w)), s2[t][:, j0 : j0 + w], ALU.mult
-                )
-            if t > 0:
-                out_of_bank(th[t - 1], t - 1, ACT.Tanh)
-        out_of_bank(th[PACK - 1], PACK - 1, ACT.Tanh)
+            for h, (src, j0, w) in enumerate(parts[t]):
+                nc.scalar.activation(th[t][:, j0 : j0 + w], src, ACT.Tanh, scale=0.0625)
+                if h == 0:
+                    nc.scalar.activation(s[t][:, j0 : j0 + w], src, ACT.Copy, scale=0.0625)
+            for src, j0, w in parts[t][1:]:
+                nc.scalar.activation(s[t][:, j0 : j0 + w], src, ACT.Copy, scale=0.0625)
+            if t < PACK - 1:
+                fused(a[t][:], th_win[t], l_n4, s[t][:], ALU.mult, t > 0)
+            else:
+                for h, (j0, w) in enumerate(O_PIECES):
+                    nc.vector.tensor_tensor(
+                        a_last[h][:], th_win[t][:].indirect(cols(l_n4, j0, w)), s[t][:, j0 : j0 + w], ALU.mult
+                    )
         for h, (j0, w) in enumerate(O_PIECES):
             o = sb(f"o{h}", [P, PACK, w], F32)
             for t in range(PACK):
-                nc.vector.tensor_tensor(o[:, t, :], th[t][:].indirect(cols(l_n4, j0, w)), a[t][:, j0 : j0 + w], ALU.mult)
-            nc.sync.dma_start(out_rows[:, :, j0 : j0 + w], o[:])
-            last = h == len(O_PIECES) - 1
-            ob = interleave(nc.vector.tensor_copy if last else nc.scalar.copy, f"ob{h}", o, w)
+                factor = a[t][:, j0 : j0 + w] if t < PACK - 1 else a_last[h][:]
+                nc.vector.tensor_tensor(o[:, t, :], s[t][:].indirect(cols(l_n3, j0, w)), factor, ALU.mult)
+                if h == 1 and t >= PACK - 2:
+                    rows = slice(0, PACK - 1) if t == PACK - 2 else slice(t, PACK)
+                    nc.sync.dma_start(out_rows[:, rows, j0 : j0 + w], o[:, rows, :])
+            if h == 0:
+                nc.sync.dma_start(out_rows[:, :, j0 : j0 + w], o[:])
+                ob = interleave(nc.scalar.copy, f"ob{h}", o, w)
+            else:
+                ob = sb(f"ob{h}", [P, w * PACK], BF16)
+                for engine_copy, c0, c1 in ((nc.scalar.copy, 0, SCALAR_COLS), (nc.vector.tensor_copy, SCALAR_COLS, w)):
+                    engine_copy(
+                        ob[:, PACK * c0 : PACK * c1].rearrange("p (c i t) -> p c t i", i=4, t=PACK),
+                        o[:, :, c0:c1].rearrange("p t (c i) -> p c t i", i=4),
+                    )
             oq = sb(f"oq{h}", [P, w], U32)
             nc.vector.quantize_mx(oq[:].bitcast(FP8X4), o_s[:, j0 : j0 + w], ob[:])
-            nc.scalar.dma_start(out_words[:, j0 : j0 + w], oq[:].bitcast(I32))
+            nc.sync.dma_start(out_words[:, j0 : j0 + w], oq[:].bitcast(I32))
         for q in range(4):
-            queue = nc.sync if q % 2 == 0 else nc.scalar
+            queue = nc.scalar if q < 3 else nc.sync
             queue.dma_start(out_2[0, 4 * q : 4 * q + 4, :].bitcast(I32), o_s[32 * q : 32 * q + 4, :].bitcast(I32))

from contextlib import ExitStack

import concourse.mybir as mybir

F32 = mybir.dt.float32
BF16 = mybir.dt.bfloat16
I32 = mybir.dt.int32
U32 = mybir.dt.uint32
U16 = mybir.dt.uint16
U8 = mybir.dt.uint8
FP8X4 = mybir.dt.float8_e4m3fn_x4
ACT = mybir.ActivationFunctionType
ALU = mybir.AluOpType

P = 128
PACK = 4
T = 2048
S = 512
HALF = S // 2
EARLY = 1
FLOPS = 2 * 2 * 512 * 512 * 512
HALVES = ((0, HALF), (HALF, HALF))
Z_PIECES = ((0, 256), (256, 128), (384, 128))
O_PIECES = HALVES
SCALAR_COLS = 96


def tile_picked_candrmscube_none_po_kernel(
    tc, x_words, x_scales, w1_words, w1_scales, gs, offs, n1, n2, cand, n3, n4, out_0, out_1, out_2
):
    nc = tc.nc
    with ExitStack() as ctx:
        keep = ctx.enter_context(tc.tile_pool(name="keep", bufs=1))
        psum = ctx.enter_context(tc.psum_pool(name="psum", bufs=1))

        def sb(name, shape, dtype, tag=None):
            return keep.tile(shape, dtype, name=name, tag=tag or name, align_bytes=64)

        def load_list(name, src):
            tile = keep.tile([P, S // 16], U16, name=name)
            nc.sync.dma_start(tile[:], src)
            return tile

        def cols(lst, j0, w):
            return lst[:, j0 // 16 : (j0 + w) // 16]

        def load_scale_rows(queue, tile, src):
            for q in range(4):
                queue.dma_start(tile[32 * q : 32 * q + 4, :].bitcast(I32), src[0, 4 * q : 4 * q + 4, :].bitcast(I32))

        def deal(dst, src, t0, t1):
            nc.vector.tensor_copy(
                dst.rearrange("p (t m) -> p t m", m=P), src.rearrange("p (m t) -> p t m", t=PACK)[:, t0:t1, :]
            )

        def deal_words(dst, src, t0, t1):
            nc.vector.tensor_copy(
                dst.rearrange("p (t m) -> p m t", m=P), src.rearrange("p (m t) -> p m t", t=PACK)[:, :, t0:t1]
            )

        def interleave(engine_copy, name, src, w):
            dst = sb(name, [P, w * PACK], BF16)
            engine_copy(
                dst[:].rearrange("p (c i t) -> p c t i", i=4, t=PACK), src[:].rearrange("p t (c i) -> p c t i", i=4)
            )
            return dst

        def chained(name):
            tiles = [sb(f"{name}{t}", [P, S if t in (0, PACK) else 2 * S], F32) for t in range(PACK + 1)]
            windows = tiles[:PACK]
            first = [tiles[t][:, 0:S] for t in range(PACK)]
            second = [tiles[t + 1][:, S : 2 * S] if t + 1 < PACK else tiles[PACK][:] for t in range(PACK)]
            return windows, first, second

        def fused(dst, window, lst, other, op, whole):
            if whole:
                nc.vector.tensor_tensor(dst, window[:].indirect(lst[:]), other, op)
            else:
                for j0, w in HALVES:
                    nc.vector.tensor_tensor(
                        dst[:, j0 : j0 + w], window[:].indirect(cols(lst, j0, w)), other[:, j0 : j0 + w], op
                    )

        def probe(name, ap, dtype):
            clock = sb(name, [P, 1], dtype)
            nc.gpsimd.tensor_copy(clock[:], ap)

        xs = sb("xs", [P, T], U8)
        ws = sb("ws", [P, S], U8)
        quarter = sb("quarter", [P, 1], F32)
        warm = sb("warm", [P, 1], F32)
        nc.gpsimd.memset(xs[:].bitcast(I32), 0)
        nc.vector.memset(ws[:].bitcast(I32), 0)
        nc.vector.memset(quarter[:], 0.25)

        ww = sb("ww", [P, S], I32)
        xw = sb("xw", [P, T], I32)
        gain = sb("gain", [P, PACK], F32)
        l_offs = load_list("l_offs", offs)
        l_cand = load_list("l_cand", cand)
        nc.sync.dma_start(ww[:], w1_words[0].rearrange("p n t -> p (n t)").bitcast(I32))
        nc.scalar.activation(warm[:], quarter[:], ACT.Abs_reciprocal_sqrt)
        load_scale_rows(nc.sync, xs, x_scales)
        nc.sync.dma_start(xw[:], x_words[0].rearrange("p n t -> p (n t)").bitcast(I32))
        load_scale_rows(nc.sync, ws, w1_scales)
        l_n1 = load_list("l_n1", n1)
        nc.sync.dma_start(gain[:], gs.rearrange("(p t) o -> p (t o)", t=PACK))
        l_n2 = load_list("l_n2", n2)
        l_n4 = load_list("l_n4", n4)
        l_n3 = load_list("l_n3", n3)

        wwd = sb("wwd", [P, S], U32)
        wsd = sb("wsd", [P, S], U8)
        deal_words(wwd[:], ww[:].bitcast(U32), 0, PACK)
        tok_s = sb("tok_s", [P, S], U8)
        tok_w = sb("tok_w", [P, S], U32)
        can_s = sb("can_s", [P, S], U8)
        nc.vector.tensor_copy(tok_s[:], xs[:].indirect(l_offs[:]))
        nc.vector.tensor_copy(can_s[:], xs[:].indirect(l_cand[:]))
        nc.vector.tensor_copy(tok_w[:], xw[:].bitcast(U32).indirect(l_offs[:]))
        deal(wsd[:], ws[:], 0, PACK)

        y_parts = []
        for t in range(PACK):
            m = slice(P * t, P * (t + 1))
            y_parts.append([])
            for h, (j0, w) in enumerate(HALVES if t == 0 else ((0, S),)):
                bank = psum.tile([P, w], F32, name=f"y_ps{t}_{h}", tag=f"bank{t + 7 * h}")
                nc.tensor.matmul_mx(
                    bank[:], lhsT=wwd[:, m].bitcast(FP8X4), lhsT_scale=wsd[:, m],
                    rhs=tok_w[:, j0 : j0 + w].bitcast(FP8X4), rhs_scale=tok_s[:, j0 : j0 + w], start=True, stop=True,
                )
                y_parts[t].append((bank[:], j0, w))

        can_w = sb("can_w", [P, S], U32, tag="ws")
        nc.vector.tensor_copy(can_w[:], xw[:].bitcast(U32).indirect(l_cand[:]))
        can_sd0 = sb("can_sd0", [P, EARLY * P], U8)
        can_wd0 = sb("can_wd0", [P, EARLY * P], U32)
        deal(can_sd0[:], can_s[:], 0, EARLY)
        deal_words(can_wd0[:], can_w[:], 0, EARLY)

        sq_win, sq, sq2 = chained("sq")
        gy = [sb(f"gy{t}", [P, S], F32) for t in range(PACK)]
        th_win = [sb(f"th{t}", [P, 2 * S], F32) for t in range(PACK)]
        th = [th_win[t][:, 0:S] for t in range(PACK)]
        den = [th_win[t][:, S : 2 * S] for t in range(PACK)]
        inv = [sb(f"inv{t}", [P, S], F32) for t in range(PACK - 1)]
        inv_last = [sb(f"inv_last{h}", [P, w], F32, tag=f"z{h + 1}") for h, (j0, w) in enumerate(Z_PIECES)]
        for t in range(PACK):
            for src, j0, w in y_parts[t]:
                nc.scalar.activation(sq[t][:, j0 : j0 + w], src, ACT.Square)
                nc.scalar.activation(sq2[t][:, j0 : j0 + w], src, ACT.Square)
        for t in range(PACK):
            fused(den[t], sq_win[t], l_n1, sq2[t], ALU.add, t > 0)
        for h, (j0, w) in enumerate(HALVES):
            for t in range(PACK):
                if h == 0:
                    for src, k0, v in y_parts[t]:
                        nc.scalar.activation(gy[t][:, k0 : k0 + v], src, ACT.Copy, scale=gain[:, t : t + 1])
                if t < PACK - 1:
                    spans = [(inv[t][:, j0 : j0 + w], j0, w)]
                else:
                    spans = [(inv_last[g][:], k0, v) for g, (k0, v) in enumerate(Z_PIECES) if j0 <= k0 < j0 + w]
                for dst, k0, v in spans:
                    nc.scalar.activation(dst, den[t][:, k0 : k0 + v], ACT.Abs_reciprocal_sqrt, bias=quarter[:])

        zq = sb("zq", [P, S], U32)
        zs = sb("zs", [P, S], U8)
        s0_ps = []
        for h, (j0, w) in enumerate(Z_PIECES):
            z = sb(f"z{h}", [P, PACK, w], F32)
            for t in range(PACK):
                factor = inv[t][:, j0 : j0 + w] if t < PACK - 1 else inv_last[h][:]
                nc.vector.tensor_tensor(z[:, t, :], gy[t][:].indirect(cols(l_n2, j0, w)), factor, ALU.mult)
            last = h == len(Z_PIECES) - 1
            zb = interleave(nc.vector.tensor_copy if last else nc.scalar.copy, f"zb{h}", z, w)
            if h == 1:
                nc.scalar.activation(warm[:], zb[:, 0:1], ACT.Tanh)
            nc.vector.quantize_mx(zq[:, j0 : j0 + w].bitcast(FP8X4), zs[:, j0 : j0 + w], zb[:])
            bank = psum.tile([P, w], F32, name=f"s0_ps{h}", tag=f"bank{PACK + h}")
            nc.tensor.matmul_mx(
                bank[:], lhsT=can_wd0[:, 0:P].bitcast(FP8X4), lhsT_scale=can_sd0[:, 0:P],
                rhs=zq[:, j0 : j0 + w].bitcast(FP8X4), rhs_scale=zs[:, j0 : j0 + w], start=True, stop=True,
            )
            s0_ps.append(bank)

        can_wd = sb("can_wd", [P, (PACK - EARLY) * P], U32, tag="zb2")
        can_sd = sb("can_sd", [P, (PACK - EARLY) * P], U8, tag="z2")
        deal(can_sd[:], can_s[:], EARLY, PACK)
        deal_words(can_wd[:], can_w[:], EARLY, PACK)
        parts = [[(s0_ps[h][:], j0, w) for h, (j0, w) in enumerate(Z_PIECES)]]
        for t in range(1, PACK):
            words, scales, u = (can_wd0, can_sd0, t) if t < EARLY else (can_wd, can_sd, t - EARLY)
            m = slice(P * u, P * (u + 1))
            bank = psum.tile([P, S], F32, name=f"s_ps{t}", tag=f"bank{t}")
            nc.tensor.matmul_mx(
                bank[:], lhsT=words[:, m].bitcast(FP8X4), lhsT_scale=scales[:, m],
                rhs=zq[:].bitcast(FP8X4), rhs_scale=zs[:], start=True, stop=True,
            )
            parts.append([(bank[:], 0, S)])
        out_rows = out_0.rearrange("(p t) j -> p t j", t=PACK)
        out_words = out_1[0].rearrange("p n t -> p (n t)").bitcast(I32)
        o_s = sb("o_s", [P, S], U8)

        s = [sb(f"s{t}", [P, S], F32) for t in range(PACK)]
        a = [sb(f"a{t}", [P, S], F32) for t in range(PACK - 1)]
        a_last = [sb(f"a_last{h}", [P, w], F32, tag=f"o{h + 1}") for h, (j0, w) in enumerate(O_PIECES)]
        for t in range(PACK):
            for h, (src, j0, w) in enumerate(parts[t]):
                nc.scalar.activation(th[t][:, j0 : j0 + w], src, ACT.Tanh, scale=0.0625)
                if h == 0:
                    nc.scalar.activation(s[t][:, j0 : j0 + w], src, ACT.Copy, scale=0.0625)
            for src, j0, w in parts[t][1:]:
                nc.scalar.activation(s[t][:, j0 : j0 + w], src, ACT.Copy, scale=0.0625)
            if t < PACK - 1:
                fused(a[t][:], th_win[t], l_n4, s[t][:], ALU.mult, t > 0)
            else:
                for h, (j0, w) in enumerate(O_PIECES):
                    nc.vector.tensor_tensor(
                        a_last[h][:], th_win[t][:].indirect(cols(l_n4, j0, w)), s[t][:, j0 : j0 + w], ALU.mult
                    )
        for h, (j0, w) in enumerate(O_PIECES):
            o = sb(f"o{h}", [P, PACK, w], F32)
            for t in range(PACK):
                factor = a[t][:, j0 : j0 + w] if t < PACK - 1 else a_last[h][:]
                nc.vector.tensor_tensor(o[:, t, :], s[t][:].indirect(cols(l_n3, j0, w)), factor, ALU.mult)
                if h == 1 and t >= PACK - 2:
                    rows = slice(0, PACK - 1) if t == PACK - 2 else slice(t, PACK)
                    nc.sync.dma_start(out_rows[:, rows, j0 : j0 + w], o[:, rows, :])
            if h == 0:
                nc.sync.dma_start(out_rows[:, :, j0 : j0 + w], o[:])
                ob = interleave(nc.scalar.copy, f"ob{h}", o, w)
            else:
                ob = sb(f"ob{h}", [P, w * PACK], BF16)
                for engine_copy, c0, c1 in ((nc.scalar.copy, 0, SCALAR_COLS), (nc.vector.tensor_copy, SCALAR_COLS, w)):
                    engine_copy(
                        ob[:, PACK * c0 : PACK * c1].rearrange("p (c i t) -> p c t i", i=4, t=PACK),
                        o[:, :, c0:c1].rearrange("p t (c i) -> p c t i", i=4),
                    )
            oq = sb(f"oq{h}", [P, w], U32)
            nc.vector.quantize_mx(oq[:].bitcast(FP8X4), o_s[:, j0 : j0 + w], ob[:])
            nc.sync.dma_start(out_words[:, j0 : j0 + w], oq[:].bitcast(I32))
        for q in range(4):
            queue = nc.scalar if q < 3 else nc.sync
            queue.dma_start(out_2[0, 4 * q : 4 * q + 4, :].bitcast(I32), o_s[32 * q : 32 * q + 4, :].bitcast(I32))
